import numpy as np
import ml_dtypes


def mxq(x, axis, fmt="e4m3"):
    dtype, down = {"e4m3": (ml_dtypes.float8_e4m3fn, 7), "e5m2": (ml_dtypes.float8_e5m2, 14)}[fmt]
    v = np.moveaxis(np.asarray(x, np.float32).astype(ml_dtypes.bfloat16).astype(np.float64), axis, -1)
    blocks = v.reshape(v.shape[:-1] + (-1, 32))
    amax = np.abs(blocks).max(-1, keepdims=True)
    byte = np.maximum(np.where(amax > 0, np.frexp(amax)[1] - 1 + 127, 0) - down, 1)
    scale = np.exp2(byte - 127.0)
    codes = (blocks / scale).astype(np.float32).astype(dtype).astype(np.float64)
    return np.moveaxis((codes * scale).reshape(v.shape), -1, axis)


WIDE = False


def mx_kscale(k):
    if not WIDE:
        return np.ones(k)
    levels = np.array([10, -10, 5, -5, 0])
    if k % 512:
        return np.exp2(np.random.permutation(np.resize(levels, k // 32))).repeat(32)
    a = np.empty((k // 512, 16))
    for p in range(k // 512):
        a[p, :8] = np.random.permutation(np.resize(levels, 8))
        for g in range(8):
            far = levels[np.abs(levels - a[p, g]) >= 10]
            a[p, g + 8] = far[np.random.randint(len(far))]
    return np.exp2(a.ravel()).repeat(32)


def f64(x):
    return np.asarray(x).astype(np.float64)


def striped(idx):
    return np.tile(idx.reshape(-1, 16).T, (8, 1)).astype(np.uint16)


def unstriped(offs):
    return offs[:16].T.reshape(-1).astype(np.int64)


def striped8(idx):
    return np.concatenate([x.reshape(-1, 16).T for x in idx]).astype(np.uint16)


def runs(offs, k):
    lists = np.stack([offs[16 * r : 16 * r + 16].T.reshape(-1) for r in range(8)]).astype(np.int64)
    return lists[np.arange(k) % 512 // 64]


def pack_weight(w):
    k, n = w.shape
    w = f64(np.asarray(w, np.float32).astype(ml_dtypes.bfloat16)).reshape(k // 32, 32, n)
    amax = np.abs(w).max(1)
    byte = np.clip(np.where(amax > 0, np.frexp(amax)[1] - 1 + 127 - 7, 1), 1, 254)
    scaled = (w * np.exp2(127.0 - byte)[:, None, :]).reshape(k, n).astype(np.float32)
    words = np.ascontiguousarray(scaled.reshape(k // 512, 128, 4, n).transpose(0, 1, 3, 2)).astype(ml_dtypes.float8_e4m3fn).view(np.uint8)
    return words, np.ascontiguousarray(byte.astype(np.uint8).reshape(k // 512, 16, n))


def unpack_weight(words, scales):
    g, p, n, _ = words.shape
    vals = np.ascontiguousarray(words).view(ml_dtypes.float8_e4m3fn).astype(np.float64) * np.repeat(np.exp2(scales.astype(np.float64) - 127.0), 8, axis=1)[..., None]
    return vals.transpose(0, 1, 3, 2).reshape(g * 512, n)


E2M1 = np.array([0.0, 0.5, 1.0, 1.5, 2.0, 3.0, 4.0, 6.0, -0.0, -0.5, -1.0, -1.5, -2.0, -3.0, -4.0, -6.0])


def pack_fp4(w):
    k, n = w.shape
    w = f64(np.asarray(w, np.float32).astype(ml_dtypes.bfloat16)).reshape(k // 32, 32, n)
    amax = np.abs(w).max(1)
    mant, ex = np.frexp(amax / 6.0)
    byte = np.clip(np.where(amax > 0, np.where(mant > 0.5, ex, ex - 1) + 127, 1), 1, 254)
    scaled = (w * np.exp2(127.0 - byte)[:, None, :]).reshape(k, n).astype(np.float32)
    c = np.ascontiguousarray(scaled.reshape(k // 512, 128, 4, n).transpose(0, 1, 3, 2)).astype(ml_dtypes.float4_e2m1fn).view(np.uint8) & 0xF
    words = (c[..., 0::2] | (c[..., 1::2] << 4)).reshape(k // 512, 128, 2 * n)
    return np.ascontiguousarray(words), np.ascontiguousarray(byte.astype(np.uint8).reshape(k // 512, 16, n))


def unpack_fp4(words, scales):
    g, _, n = scales.shape
    words = np.ascontiguousarray(words).reshape(g, 128, n, 2)
    nib = np.empty((g, 128, n, 4), np.uint8)
    nib[..., 0::2] = words & 0xF
    nib[..., 1::2] = words >> 4
    vals = E2M1[nib] * np.repeat(np.exp2(scales.astype(np.float64) - 127.0), 8, axis=1)[..., None]
    return vals.transpose(0, 1, 3, 2).reshape(g * 512, n)


def planes(y):
    n, m = y.shape
    v = y.astype(np.float32).astype(ml_dtypes.bfloat16).astype(np.float64).reshape(n // 32, 32, m)
    top = np.abs(v).max(1)
    byte = np.clip(np.where(top > 0, np.frexp(top)[1] - 1 + 127 - 7, 1), 1, 254)
    codes = (v * np.exp2(127.0 - byte)[:, None, :]).reshape(n, m).astype(np.float32).astype(ml_dtypes.float8_e4m3fn).view(np.uint8)
    words = codes.reshape(n // 512, 128, 4, m).transpose(0, 1, 3, 2)
    return np.ascontiguousarray(words), np.ascontiguousarray(byte.astype(np.uint8).reshape(n // 512, 16, m))


K, T, S, H, C, W = 512, 2048, 256, 512, 512, 1024


def setup_inputs():
    n = np.random.standard_normal
    s = mx_kscale(K)[:, None]
    packed_xT = pack_weight(n((K, T)) * s)
    packed_w1 = pack_fp4(n((K, H)) / np.sqrt(K) / s)
    return {
        "x_words": packed_xT[0],
        "x_scales": packed_xT[1],
        "w1_words": packed_w1[0],
        "w1_scales": packed_w1[1],
        "gs": (np.random.uniform(0.5, 1.5, (K, 1)) / s).astype(np.float32),
        "offs": striped(np.random.permutation(T)[:S]),
        "n1": striped8(np.stack([np.random.permutation(S) for _ in range(8)])),
        "n2": striped8(np.stack([np.random.permutation(S) for _ in range(8)])),
        "cand": striped(np.random.permutation(T)[:C]),
        "n3": striped(np.random.randint(0, S, W)),
    }


def reference(x_words, x_scales, w1_words, w1_scales, gs, offs, n1, n2, cand, n3):
    x_cand = unpack_weight(x_words, x_scales)[:, unstriped(cand)]
    xq = unpack_weight(x_words, x_scales)[:, unstriped(offs)]
    y = unpack_fp4(w1_words, w1_scales).T @ xq
    z = f64(gs) * (y - (np.minimum(y[np.arange(H)[:, None], runs(n1, H)], y[np.arange(H)[:, None], runs(n2, H)])))
    s = 0.0625 * ((x_cand.T @ mxq(z, 0, "e4m3")))
    mb = s[:, unstriped(n3)]
    mx = mb.reshape(C, S, 4).max(axis=2)
    mn = mb.reshape(C, S, 4).min(axis=2)
    out_0 = mx - (0.5 * mn)
    return (out_0,) + planes(out_0)

@@ -1,0 +1,172 @@
+from contextlib import ExitStack
+
+import concourse.mybir as mybir
+
+K, T, S, H, C, W = 512, 2048, 256, 512, 512, 1024
+FLOPS = 2 * K * H * S + 2 * K * C * S
+
+F32 = mybir.dt.float32
+BF16 = mybir.dt.bfloat16
+I32 = mybir.dt.int32
+U32 = mybir.dt.uint32
+U16 = mybir.dt.uint16
+U8 = mybir.dt.uint8
+FP8X4 = mybir.dt.float8_e4m3fn_x4
+FP4X4 = mybir.dt.float4_e2m1fn_x4
+ALU = mybir.AluOpType
+COPY = mybir.ActivationFunctionType.Copy
+
+P = 128
+PACK = 4
+MEMBERS = 4
+Z_CHUNKS = ((0, 128), (128, 64), (192, 64))
+OUT_COLS = 64
+S_WINDOW = S + 16
+
+
+def tile_picked_candundergspan_none_po_kernel(
+    tc, x_words, x_scales, w1_words, w1_scales, gs, offs, n1, n2, cand, n3, out_0, out_1, out_2
+):
+    nc = tc.nc
+    with ExitStack() as ctx:
+        keep = ctx.enter_context(tc.tile_pool(name="keep", bufs=1))
+        psum = ctx.enter_context(tc.psum_pool(name="psum", bufs=1))
+
+        offs_sb = keep.tile([P, S // 16], U16, name="offs_sb")
+        cand_sb = keep.tile([P, C // 16], U16, name="cand_sb")
+        n1_sb = keep.tile([P, S // 16], U16, name="n1_sb")
+        n2_sb = keep.tile([P, S // 16], U16, name="n2_sb")
+        n3_sb = keep.tile([P, W // 16], U16, name="n3_sb")
+        x_tab = keep.tile([P, T], I32, name="x_tab", align_bytes=64)
+        xs_tab = keep.tile([P, T], U8, name="xs_tab", align_bytes=64)
+        w_raw = keep.tile([P, 2 * H], U8, name="w_raw", align_bytes=64)
+        ws_raw = keep.tile([P, H], U8, name="ws_raw", align_bytes=64)
+        gs_sb = keep.tile([P, PACK], F32, name="gs_sb")
+
+        nc.vector.memset(xs_tab[:].bitcast(I32), 0)
+        nc.vector.memset(ws_raw[:].bitcast(I32), 0)
+        nc.sync.dma_start(offs_sb[:], offs)
+        nc.sync.dma_start(cand_sb[:], cand)
+        nc.sync.dma_start(n1_sb[:], n1)
+        nc.sync.dma_start(n2_sb[:], n2)
+        nc.sync.dma_start(x_tab[:], x_words[0].rearrange("p n t -> p (n t)").bitcast(I32))
+        nc.scalar.dma_start(w_raw[:].bitcast(I32), w1_words[0].bitcast(I32))
+        for q in range(4):
+            nc.scalar.dma_start(xs_tab[32 * q : 32 * q + 4, :].bitcast(I32), x_scales[0, 4 * q : 4 * q + 4, :].bitcast(I32))
+        for q in range(4):
+            nc.scalar.dma_start(ws_raw[32 * q : 32 * q + 4, :].bitcast(I32), w1_scales[0, 4 * q : 4 * q + 4, :].bitcast(I32))
+        nc.gpsimd.dma_start(gs_sb[:], gs.rearrange("(p t) o -> p (t o)", t=PACK))
+        nc.sync.dma_start(n3_sb[:], n3)
+
+        s_sb = [keep.tile([P, S_WINDOW], F32, name="s_sb%d" % t) for t in range(PACK)]
+        for t in range(PACK):
+            nc.gpsimd.memset(s_sb[t][:, S:], 0.0)
+
+        xq_s = keep.tile([P, S], U8, name="xq_s", align_bytes=64)
+        xq_w = keep.tile([P, S], U32, name="xq_w", align_bytes=64)
+        w_deal = keep.tile([P, 2 * H], U8, name="w_deal", align_bytes=64)
+        ws_deal = keep.tile([P, H], U8, name="ws_deal", align_bytes=64)
+        nc.vector.tensor_copy(xq_s[:], xs_tab[:].indirect(offs_sb[:]))
+        nc.vector.tensor_copy(
+            w_deal[:].rearrange("p (t m b) -> p t m b", t=PACK, b=2), w_raw[:].rearrange("p (m t b) -> p t m b", t=PACK, b=2)
+        )
+        nc.vector.tensor_copy(ws_deal[:].rearrange("p (t m) -> p t m", t=PACK), ws_raw[:].rearrange("p (m t) -> p t m", t=PACK))
+        nc.vector.tensor_copy(xq_w[:], x_tab[:].bitcast(U32).indirect(offs_sb[:]))
+
+        y_sb = [keep.tile([P, S], F32, name="y_sb%d" % t) for t in range(PACK)]
+        y_ps = [psum.tile([P, S], F32, name="y_ps%d" % t) for t in range(PACK)]
+        for t in range(PACK):
+            nc.tensor.matmul_mx(
+                out=y_ps[t][:],
+                lhsT=w_deal[:, 2 * P * t : 2 * P * (t + 1)].bitcast(FP4X4),
+                lhsT_scale=ws_deal[:, P * t : P * (t + 1)],
+                rhs=xq_w[:].bitcast(FP8X4),
+                rhs_scale=xq_s[:],
+                start=True,
+                stop=True,
+            )
+        nc.scalar.copy(y_sb[0][:], y_ps[0][:])
+        for t in range(1, PACK):
+            nc.vector.tensor_copy(y_sb[t][:], y_ps[t][:])
+
+        xc_s = keep.tile([P, C], U8, name="xc_s", align_bytes=64)
+        xc_w = keep.tile([P, C], U32, name="xc_w", align_bytes=64)
+        cs_deal = keep.tile([P, C], U8, name="cs_deal", align_bytes=64)
+        cw_deal = keep.tile([P, C], U32, name="cw_deal", align_bytes=64)
+        nc.vector.tensor_copy(xc_s[:], xs_tab[:].indirect(cand_sb[:]))
+        nc.vector.tensor_copy(cs_deal[:].rearrange("p (t m) -> p t m", t=PACK), xc_s[:].rearrange("p (m t) -> p t m", t=PACK))
+        half = C // 2
+        for h in range(2):
+            nc.vector.tensor_copy(
+                xc_w[:, half * h : half * (h + 1)], x_tab[:].bitcast(U32).indirect(cand_sb[:, half // 16 * h : half // 16 * (h + 1)])
+            )
+        nc.vector.tensor_copy(cw_deal[:].rearrange("p (t m) -> p t m", t=PACK), xc_w[:].rearrange("p (m t) -> p t m", t=PACK))
+
+        z_w = keep.tile([P, S], U32, name="z_w", align_bytes=64)
+        z_s = keep.tile([P, S], U8, name="z_s", align_bytes=64)
+        s_ps = [psum.tile([P, S], F32, name="s_ps%d" % t) for t in range(PACK)]
+        for c0, n in Z_CHUNKS:
+            cols = slice(c0, c0 + n)
+            lists = slice(c0 // 16, (c0 + n) // 16)
+            near = keep.tile([P, PACK, 2, n], F32, name="near%d" % c0)
+            low = keep.tile([P, PACK, n], F32, name="low%d" % c0)
+            diff = keep.tile([P, PACK, n], F32, name="diff%d" % c0)
+            z_bf = keep.tile([P, n, PACK], BF16, name="z_bf%d" % c0, align_bytes=64)
+            for t in range(PACK):
+                nc.scalar.activation(near[:, t, 0, :], y_sb[t][:].indirect(n1_sb[:, lists]), COPY)
+                nc.scalar.activation(near[:, t, 1, :], y_sb[t][:].indirect(n2_sb[:, lists]), COPY)
+                nc.vector.tensor_tensor(low[:, t, :], near[:, t, 0, :], near[:, t, 1, :], ALU.min)
+                nc.vector.tensor_tensor(diff[:, t, :], y_sb[t][:, cols], low[:, t, :], ALU.subtract)
+            nc.vector.tensor_tensor(
+                z_bf[:], diff[:].rearrange("p t j -> p j t"), gs_sb[:].unsqueeze(1).to_broadcast([P, n, PACK]), ALU.mult
+            )
+            nc.vector.quantize_mx(out=z_w[:, cols].bitcast(FP8X4), scales=z_s[:, cols], in_=z_bf[:].rearrange("p j t -> p (j t)"))
+            for t in range(PACK):
+                nc.tensor.matmul_mx(
+                    out=s_ps[t][:, cols],
+                    lhsT=cw_deal[:, P * t : P * (t + 1)].bitcast(FP8X4),
+                    lhsT_scale=cs_deal[:, P * t : P * (t + 1)],
+                    rhs=z_w[:, cols].bitcast(FP8X4),
+                    rhs_scale=z_s[:, cols],
+                    start=True,
+                    stop=True,
+                )
+        last0 = Z_CHUNKS[-1][0]
+        for c0, n in Z_CHUNKS[:-1]:
+            for t in range(PACK):
+                nc.scalar.activation(s_sb[t][:, c0 : c0 + n], s_ps[t][:, c0 : c0 + n], COPY, scale=0.0625)
+        for t in range(PACK):
+            nc.vector.tensor_scalar(s_sb[t][:, last0:S], s_ps[t][:, last0:S], 0.0625, None, ALU.mult)
+
+        o_w = keep.tile([P, S], U32, name="o_w", align_bytes=64)
+        o_s = keep.tile([P, S], U8, name="o_s", align_bytes=64)
+        out_rows = out_0.rearrange("(p t) j -> p t j", t=PACK)
+        out_words = out_1[0].rearrange("p n t -> p (n t)").bitcast(I32)
+        n = OUT_COLS
+        for c0 in range(0, S, n):
+            cols = slice(c0, c0 + n)
+            lists = slice(c0 * MEMBERS // 16, (c0 + n) * MEMBERS // 16)
+            mb = keep.tile([P, PACK, n, MEMBERS], F32, name="mb%d" % c0)
+            hi = keep.tile([P, PACK, n, 2], F32, name="hi%d" % c0)
+            lo = keep.tile([P, PACK, n, 2], F32, name="lo%d" % c0)
+            mx = keep.tile([P, PACK, n], F32, name="mx%d" % c0)
+            mn = keep.tile([P, PACK, n], F32, name="mn%d" % c0)
+            res = keep.tile([P, PACK, n], F32, name="res%d" % c0)
+            res_bf = keep.tile([P, n, PACK], BF16, name="res_bf%d" % c0, align_bytes=64)
+            groups = ((0, 2), (2, 4)) if c0 + n < S else ((0, 2), (2, 3), (3, 4))
+            for t0, t1 in groups:
+                for t in range(t0, t1):
+                    nc.scalar.activation(mb[:, t].rearrange("p j m -> p (j m)"), s_sb[t][:].indirect(n3_sb[:, lists]), COPY)
+                ts = slice(t0, t1)
+                nc.vector.tensor_tensor(hi[:, ts], mb[:, ts, :, 0:2], mb[:, ts, :, 2:4], ALU.max)
+                nc.vector.tensor_tensor(lo[:, ts], mb[:, ts, :, 0:2], mb[:, ts, :, 2:4], ALU.min)
+                nc.vector.tensor_tensor(mx[:, ts], hi[:, ts, :, 0], hi[:, ts, :, 1], ALU.max)
+                nc.vector.tensor_tensor(mn[:, ts], lo[:, ts, :, 0], lo[:, ts, :, 1], ALU.min)
+                nc.vector.scalar_tensor_tensor(res[:, ts], mn[:, ts], -0.5, mx[:, ts], ALU.mult, ALU.add)
+            nc.sync.dma_start(out_rows[:, :, cols], res[:])
+            nc.vector.tensor_copy(res_bf[:], res[:].rearrange("p t j -> p j t"))
+            nc.vector.quantize_mx(out=o_w[:, cols].bitcast(FP8X4), scales=o_s[:, cols], in_=res_bf[:].rearrange("p j t -> p (j t)"))
+            nc.sync.dma_start(out_words[:, cols], o_w[:, cols].bitcast(I32))
+        for q in range(4):
+            eng = nc.sync if q % 2 else nc.scalar
+            eng.dma_start(out_2[0, 4 * q : 4 * q + 4, :].bitcast(I32), o_s[32 * q : 32 * q + 4, :].bitcast(I32))

@@ -19,9 +19,9 @@ COPY = mybir.ActivationFunctionType.Copy
 P = 128
 PACK = 4
 MEMBERS = 4
-Z_CHUNKS = ((0, 128), (128, 64), (192, 64))
-OUT_COLS = 64
-S_WINDOW = S + 16
+Z_CHUNKS = ((0, 128), (128, 128))
+OUT_CHUNKS = ((0, 128), (128, 64), (192, 64))
+S_WINDOW = 512 + 16
 
 
 def tile_picked_candundergspan_none_po_kernel(
@@ -40,68 +40,69 @@ def tile_picked_candundergspan_none_po_kernel(
         x_tab = keep.tile([P, T], I32, name="x_tab", align_bytes=64)
         xs_tab = keep.tile([P, T], U8, name="xs_tab", align_bytes=64)
         w_raw = keep.tile([P, 2 * H], U8, name="w_raw", align_bytes=64)
-        ws_raw = keep.tile([P, H], U8, name="ws_raw", align_bytes=64)
         gs_sb = keep.tile([P, PACK], F32, name="gs_sb")
+        ws_raw = keep.tile([P, H], U8, name="ws_raw", align_bytes=64)
 
+        nc.gpsimd.memset(ws_raw[:].bitcast(I32), 0)
         nc.vector.memset(xs_tab[:].bitcast(I32), 0)
-        nc.vector.memset(ws_raw[:].bitcast(I32), 0)
         nc.sync.dma_start(offs_sb[:], offs)
+        nc.sync.dma_start(w_raw[:].bitcast(I32), w1_words[0].bitcast(I32))
         nc.sync.dma_start(cand_sb[:], cand)
-        nc.sync.dma_start(n1_sb[:], n1)
-        nc.sync.dma_start(n2_sb[:], n2)
         nc.sync.dma_start(x_tab[:], x_words[0].rearrange("p n t -> p (n t)").bitcast(I32))
-        nc.scalar.dma_start(w_raw[:].bitcast(I32), w1_words[0].bitcast(I32))
-        for q in range(4):
-            nc.scalar.dma_start(xs_tab[32 * q : 32 * q + 4, :].bitcast(I32), x_scales[0, 4 * q : 4 * q + 4, :].bitcast(I32))
+        for tile_sb, src in ((n1_sb, n1), (n2_sb, n2), (n3_sb, n3)):
+            nc.sync.dma_start(tile_sb[:], src)
+        nc.sync.dma_start(gs_sb[:], gs.rearrange("(p t) o -> p (t o)", t=PACK))
         for q in range(4):
             nc.scalar.dma_start(ws_raw[32 * q : 32 * q + 4, :].bitcast(I32), w1_scales[0, 4 * q : 4 * q + 4, :].bitcast(I32))
-        nc.gpsimd.dma_start(gs_sb[:], gs.rearrange("(p t) o -> p (t o)", t=PACK))
-        nc.sync.dma_start(n3_sb[:], n3)
+        for q in range(4):
+            nc.scalar.dma_start(xs_tab[32 * q : 32 * q + 4, :].bitcast(I32), x_scales[0, 4 * q : 4 * q + 4, :].bitcast(I32))
 
         s_sb = [keep.tile([P, S_WINDOW], F32, name="s_sb%d" % t) for t in range(PACK)]
         for t in range(PACK):
-            nc.gpsimd.memset(s_sb[t][:, S:], 0.0)
+            nc.vector.memset(s_sb[t][:, S:], 0.0)
 
         xq_s = keep.tile([P, S], U8, name="xq_s", align_bytes=64)
         xq_w = keep.tile([P, S], U32, name="xq_w", align_bytes=64)
-        w_deal = keep.tile([P, 2 * H], U8, name="w_deal", align_bytes=64)
-        ws_deal = keep.tile([P, H], U8, name="ws_deal", align_bytes=64)
-        nc.vector.tensor_copy(xq_s[:], xs_tab[:].indirect(offs_sb[:]))
-        nc.vector.tensor_copy(
-            w_deal[:].rearrange("p (t m b) -> p t m b", t=PACK, b=2), w_raw[:].rearrange("p (m t b) -> p t m b", t=PACK, b=2)
-        )
+        w_first = keep.tile([P, 2 * P], U8, name="w_first", tag="scales_then_words", align_bytes=64)
+        w_rest = keep.tile([P, PACK - 1, 2 * P], U8, name="w_rest", align_bytes=64)
+        w_deal = [w_first[:]] + [w_rest[:, t] for t in range(PACK - 1)]
+        ws_deal = keep.tile([P, H], U8, name="ws_deal", tag="dealt_then_picked", align_bytes=64)
+        w_cols = w_raw[:].rearrange("p (m t b) -> p t m b", t=PACK, b=2)
+        nc.vector.tensor_copy(w_first[:].rearrange("p (m b) -> p m b", b=2), w_cols[:, 0])
+        nc.vector.tensor_copy(w_rest[:].rearrange("p t (m b) -> p t m b", b=2), w_cols[:, 1:])
         nc.vector.tensor_copy(ws_deal[:].rearrange("p (t m) -> p t m", t=PACK), ws_raw[:].rearrange("p (m t) -> p t m", t=PACK))
         nc.vector.tensor_copy(xq_w[:], x_tab[:].bitcast(U32).indirect(offs_sb[:]))
+        nc.vector.tensor_copy(xq_s[:], xs_tab[:].indirect(offs_sb[:]))
 
         y_sb = [keep.tile([P, S], F32, name="y_sb%d" % t) for t in range(PACK)]
         y_ps = [psum.tile([P, S], F32, name="y_ps%d" % t) for t in range(PACK)]
         for t in range(PACK):
             nc.tensor.matmul_mx(
                 out=y_ps[t][:],
-                lhsT=w_deal[:, 2 * P * t : 2 * P * (t + 1)].bitcast(FP4X4),
+                lhsT=w_deal[t].bitcast(FP4X4),
                 lhsT_scale=ws_deal[:, P * t : P * (t + 1)],
                 rhs=xq_w[:].bitcast(FP8X4),
                 rhs_scale=xq_s[:],
                 start=True,
                 stop=True,
             )
-        nc.scalar.copy(y_sb[0][:], y_ps[0][:])
-        for t in range(1, PACK):
-            nc.vector.tensor_copy(y_sb[t][:], y_ps[t][:])
+        for t in range(PACK):
+            nc.scalar.copy(y_sb[t][:], y_ps[t][:])
 
-        xc_s = keep.tile([P, C], U8, name="xc_s", align_bytes=64)
-        xc_w = keep.tile([P, C], U32, name="xc_w", align_bytes=64)
+        xc_s = keep.tile([P, C], U8, name="xc_s", tag="dealt_then_picked", align_bytes=64)
+        xc_w = keep.tile([P, C], U32, name="xc_w", tag="scales_then_words", align_bytes=64)
         cs_deal = keep.tile([P, C], U8, name="cs_deal", align_bytes=64)
         cw_deal = keep.tile([P, C], U32, name="cw_deal", align_bytes=64)
+        nc.vector.tensor_copy(xc_w[:], x_tab[:].bitcast(U32).indirect(cand_sb[:]))
         nc.vector.tensor_copy(xc_s[:], xs_tab[:].indirect(cand_sb[:]))
-        nc.vector.tensor_copy(cs_deal[:].rearrange("p (t m) -> p t m", t=PACK), xc_s[:].rearrange("p (m t) -> p t m", t=PACK))
-        half = C // 2
-        for h in range(2):
-            nc.vector.tensor_copy(
-                xc_w[:, half * h : half * (h + 1)], x_tab[:].bitcast(U32).indirect(cand_sb[:, half // 16 * h : half // 16 * (h + 1)])
-            )
         nc.vector.tensor_copy(cw_deal[:].rearrange("p (t m) -> p t m", t=PACK), xc_w[:].rearrange("p (m t) -> p t m", t=PACK))
+        nc.vector.tensor_copy(cs_deal[:].rearrange("p (t m) -> p t m", t=PACK), xc_s[:].rearrange("p (m t) -> p t m", t=PACK))
 
+        last0, last_n = Z_CHUNKS[-1]
+        neg_gs = keep.tile([P, 1], F32, name="neg_gs")
+        gy_last = keep.tile([P, last_n], F32, name="gy_last")
+        nc.vector.tensor_scalar(neg_gs[:], gs_sb[:, PACK - 1 : PACK], -1.0, None, ALU.mult)
+        nc.vector.tensor_scalar(gy_last[:], y_sb[PACK - 1][:, last0:], gs_sb[:, PACK - 1 : PACK], None, ALU.mult)
         z_w = keep.tile([P, S], U32, name="z_w", align_bytes=64)
         z_s = keep.tile([P, S], U8, name="z_s", align_bytes=64)
         s_ps = [psum.tile([P, S], F32, name="s_ps%d" % t) for t in range(PACK)]
@@ -109,17 +110,27 @@ def tile_picked_candundergspan_none_po_kernel(
             cols = slice(c0, c0 + n)
             lists = slice(c0 // 16, (c0 + n) // 16)
             near = keep.tile([P, PACK, 2, n], F32, name="near%d" % c0)
-            low = keep.tile([P, PACK, n], F32, name="low%d" % c0)
-            diff = keep.tile([P, PACK, n], F32, name="diff%d" % c0)
+            low = keep.tile([P, PACK, n], F32, name="low", tag="low")
             z_bf = keep.tile([P, n, PACK], BF16, name="z_bf%d" % c0, align_bytes=64)
-            for t in range(PACK):
-                nc.scalar.activation(near[:, t, 0, :], y_sb[t][:].indirect(n1_sb[:, lists]), COPY)
-                nc.scalar.activation(near[:, t, 1, :], y_sb[t][:].indirect(n2_sb[:, lists]), COPY)
-                nc.vector.tensor_tensor(low[:, t, :], near[:, t, 0, :], near[:, t, 1, :], ALU.min)
-                nc.vector.tensor_tensor(diff[:, t, :], y_sb[t][:, cols], low[:, t, :], ALU.subtract)
-            nc.vector.tensor_tensor(
-                z_bf[:], diff[:].rearrange("p t j -> p j t"), gs_sb[:].unsqueeze(1).to_broadcast([P, n, PACK]), ALU.mult
-            )
+            groups = ((0, 2), (2, 4)) if c0 + n < S else ((0, 2), (2, 3), (3, 4))
+            for t0, t1 in groups:
+                for t in range(t0, t1):
+                    nc.scalar.activation(near[:, t, 0, :], y_sb[t][:].indirect(n1_sb[:, lists]), COPY)
+                    nc.scalar.activation(near[:, t, 1, :], y_sb[t][:].indirect(n2_sb[:, lists]), COPY)
+                nc.vector.tensor_tensor(low[:, t0:t1, :], near[:, t0:t1, 0, :], near[:, t0:t1, 1, :], ALU.min)
+                if c0 == last0 and t1 == PACK:
+                    nc.vector.scalar_tensor_tensor(z_bf[:, :, t0], low[:, t0, :], neg_gs[:], gy_last[:], ALU.mult, ALU.add)
+                    continue
+                for t in range(t0, t1):
+                    nc.vector.tensor_tensor(low[:, t, :], y_sb[t][:, cols], low[:, t, :], ALU.subtract)
+                tn = PACK - 1 if c0 == last0 else PACK
+                if t1 == tn:
+                    nc.vector.tensor_tensor(
+                        z_bf[:, :, :tn],
+                        low[:, :tn].rearrange("p t j -> p j t"),
+                        gs_sb[:, :tn].unsqueeze(1).to_broadcast([P, n, tn]),
+                        ALU.mult,
+                    )
             nc.vector.quantize_mx(out=z_w[:, cols].bitcast(FP8X4), scales=z_s[:, cols], in_=z_bf[:].rearrange("p j t -> p (j t)"))
             for t in range(PACK):
                 nc.tensor.matmul_mx(
@@ -131,7 +142,6 @@ def tile_picked_candundergspan_none_po_kernel(
                     start=True,
                     stop=True,
                 )
-        last0 = Z_CHUNKS[-1][0]
         for c0, n in Z_CHUNKS[:-1]:
             for t in range(PACK):
                 nc.scalar.activation(s_sb[t][:, c0 : c0 + n], s_ps[t][:, c0 : c0 + n], COPY, scale=0.0625)
@@ -142,8 +152,7 @@ def tile_picked_candundergspan_none_po_kernel(
         o_s = keep.tile([P, S], U8, name="o_s", align_bytes=64)
         out_rows = out_0.rearrange("(p t) j -> p t j", t=PACK)
         out_words = out_1[0].rearrange("p n t -> p (n t)").bitcast(I32)
-        n = OUT_COLS
-        for c0 in range(0, S, n):
+        for c0, n in OUT_CHUNKS:
             cols = slice(c0, c0 + n)
             lists = slice(c0 * MEMBERS // 16, (c0 + n) * MEMBERS // 16)
             mb = keep.tile([P, PACK, n, MEMBERS], F32, name="mb%d" % c0)
@@ -153,18 +162,26 @@ def tile_picked_candundergspan_none_po_kernel(
             mn = keep.tile([P, PACK, n], F32, name="mn%d" % c0)
             res = keep.tile([P, PACK, n], F32, name="res%d" % c0)
             res_bf = keep.tile([P, n, PACK], BF16, name="res_bf%d" % c0, align_bytes=64)
-            groups = ((0, 2), (2, 4)) if c0 + n < S else ((0, 2), (2, 3), (3, 4))
-            for t0, t1 in groups:
-                for t in range(t0, t1):
-                    nc.scalar.activation(mb[:, t].rearrange("p j m -> p (j m)"), s_sb[t][:].indirect(n3_sb[:, lists]), COPY)
-                ts = slice(t0, t1)
-                nc.vector.tensor_tensor(hi[:, ts], mb[:, ts, :, 0:2], mb[:, ts, :, 2:4], ALU.max)
-                nc.vector.tensor_tensor(lo[:, ts], mb[:, ts, :, 0:2], mb[:, ts, :, 2:4], ALU.min)
+            pair_groups = ((0, 1), (1, 2), (2, 3), (3, 4)) if n == 128 else ((0, 2), (2, 4)) if c0 + n < S else ((0, 2), (2, 3), (3, 4))
+            end_groups = ((0, 2), (2, 4)) if n == 128 else ((0, 4),) if c0 + n < S else ((0, 3), (3, 4))
+            for e0, e1 in end_groups:
+                for t0, t1 in pair_groups:
+                    if e0 <= t0 < e1:
+                        for t in range(t0, t1):
+                            nc.scalar.activation(mb[:, t].rearrange("p j m -> p (j m)"), s_sb[t][:].indirect(n3_sb[:, lists]), COPY)
+                        ts = slice(t0, t1)
+                        nc.vector.tensor_tensor(hi[:, ts], mb[:, ts, :, 0:2], mb[:, ts, :, 2:4], ALU.max)
+                        nc.vector.tensor_tensor(lo[:, ts], mb[:, ts, :, 0:2], mb[:, ts, :, 2:4], ALU.min)
+                ts = slice(e0, e1)
                 nc.vector.tensor_tensor(mx[:, ts], hi[:, ts, :, 0], hi[:, ts, :, 1], ALU.max)
                 nc.vector.tensor_tensor(mn[:, ts], lo[:, ts, :, 0], lo[:, ts, :, 1], ALU.min)
+                if c0 + n == S and e1 == PACK:
+                    nc.vector.scalar_tensor_tensor(res_bf[:, :, e0], mn[:, e0], -0.5, mx[:, e0], ALU.mult, ALU.add)
                 nc.vector.scalar_tensor_tensor(res[:, ts], mn[:, ts], -0.5, mx[:, ts], ALU.mult, ALU.add)
+                tn = PACK - 1 if c0 + n == S else PACK
+                if e1 == tn:
+                    nc.vector.tensor_copy(res_bf[:, :, :tn], res[:, :tn].rearrange("p t j -> p j t"))
             nc.sync.dma_start(out_rows[:, :, cols], res[:])
-            nc.vector.tensor_copy(res_bf[:], res[:].rearrange("p t j -> p j t"))
             nc.vector.quantize_mx(out=o_w[:, cols].bitcast(FP8X4), scales=o_s[:, cols], in_=res_bf[:].rearrange("p j t -> p (j t)"))
             nc.sync.dma_start(out_words[:, cols], o_w[:, cols].bitcast(I32))
         for q in range(4):

@@ -20,7 +20,7 @@ P = 128
 PACK = 4
 MEMBERS = 4
 Z_CHUNKS = ((0, 128), (128, 128))
-OUT_CHUNKS = ((0, 128), (128, 64), (192, 64))
+OUT_CHUNKS = ((0, 64), (64, 128), (192, 64))
 S_WINDOW = 512 + 16
 
 
@@ -43,8 +43,9 @@ def tile_picked_candundergspan_none_po_kernel(
         gs_sb = keep.tile([P, PACK], F32, name="gs_sb")
         ws_raw = keep.tile([P, H], U8, name="ws_raw", align_bytes=64)
 
+        nc.vector.memset(xs_tab[:, : T // 2].bitcast(I32), 0)
+        nc.gpsimd.memset(xs_tab[:, T // 2 :].bitcast(I32), 0)
         nc.gpsimd.memset(ws_raw[:].bitcast(I32), 0)
-        nc.vector.memset(xs_tab[:].bitcast(I32), 0)
         nc.sync.dma_start(offs_sb[:], offs)
         nc.sync.dma_start(w_raw[:].bitcast(I32), w1_words[0].bitcast(I32))
         nc.sync.dma_start(cand_sb[:], cand)
@@ -53,28 +54,31 @@ def tile_picked_candundergspan_none_po_kernel(
             nc.sync.dma_start(tile_sb[:], src)
         nc.sync.dma_start(gs_sb[:], gs.rearrange("(p t) o -> p (t o)", t=PACK))
         for q in range(4):
-            nc.scalar.dma_start(ws_raw[32 * q : 32 * q + 4, :].bitcast(I32), w1_scales[0, 4 * q : 4 * q + 4, :].bitcast(I32))
-        for q in range(4):
             nc.scalar.dma_start(xs_tab[32 * q : 32 * q + 4, :].bitcast(I32), x_scales[0, 4 * q : 4 * q + 4, :].bitcast(I32))
+        for q in range(4):
+            nc.scalar.dma_start(ws_raw[32 * q : 32 * q + 4, :].bitcast(I32), w1_scales[0, 4 * q : 4 * q + 4, :].bitcast(I32))
 
         s_sb = [keep.tile([P, S_WINDOW], F32, name="s_sb%d" % t) for t in range(PACK)]
         for t in range(PACK):
-            nc.vector.memset(s_sb[t][:, S:], 0.0)
+            nc.gpsimd.memset(s_sb[t][:, S:], 0.0)
 
         xq_s = keep.tile([P, S], U8, name="xq_s", align_bytes=64)
         xq_w = keep.tile([P, S], U32, name="xq_w", align_bytes=64)
         w_first = keep.tile([P, 2 * P], U8, name="w_first", tag="scales_then_words", align_bytes=64)
         w_rest = keep.tile([P, PACK - 1, 2 * P], U8, name="w_rest", align_bytes=64)
         w_deal = [w_first[:]] + [w_rest[:, t] for t in range(PACK - 1)]
-        ws_deal = keep.tile([P, H], U8, name="ws_deal", tag="dealt_then_picked", align_bytes=64)
+        ws_deal = keep.tile([P, H], U8, name="ws_deal", align_bytes=64)
         w_cols = w_raw[:].rearrange("p (m t b) -> p t m b", t=PACK, b=2)
         nc.vector.tensor_copy(w_first[:].rearrange("p (m b) -> p m b", b=2), w_cols[:, 0])
         nc.vector.tensor_copy(w_rest[:].rearrange("p t (m b) -> p t m b", b=2), w_cols[:, 1:])
         nc.vector.tensor_copy(ws_deal[:].rearrange("p (t m) -> p t m", t=PACK), ws_raw[:].rearrange("p (m t) -> p t m", t=PACK))
-        nc.vector.tensor_copy(xq_w[:], x_tab[:].bitcast(U32).indirect(offs_sb[:]))
         nc.vector.tensor_copy(xq_s[:], xs_tab[:].indirect(offs_sb[:]))
+        nc.vector.tensor_copy(xq_w[:], x_tab[:].bitcast(U32).indirect(offs_sb[:]))
 
-        y_sb = [keep.tile([P, S], F32, name="y_sb%d" % t) for t in range(PACK)]
+        last_t = PACK - 1
+        y_sb = [keep.tile([P, 2 * S if t < last_t else S], F32, name="y_sb%d" % t) for t in range(PACK)]
+        for t in range(last_t):
+            nc.vector.memset(y_sb[t][:, S:], 0.0)
         y_ps = [psum.tile([P, S], F32, name="y_ps%d" % t) for t in range(PACK)]
         for t in range(PACK):
             nc.tensor.matmul_mx(
@@ -87,9 +91,12 @@ def tile_picked_candundergspan_none_po_kernel(
                 stop=True,
             )
         for t in range(PACK):
-            nc.scalar.copy(y_sb[t][:], y_ps[t][:])
+            if t < 2:
+                nc.scalar.copy(y_sb[t][:, :S], y_ps[t][:])
+            else:
+                nc.vector.tensor_copy(y_sb[t][:, :S], y_ps[t][:])
 
-        xc_s = keep.tile([P, C], U8, name="xc_s", tag="dealt_then_picked", align_bytes=64)
+        xc_s = keep.tile([P, C], U8, name="xc_s", align_bytes=64)
         xc_w = keep.tile([P, C], U32, name="xc_w", tag="scales_then_words", align_bytes=64)
         cs_deal = keep.tile([P, C], U8, name="cs_deal", align_bytes=64)
         cw_deal = keep.tile([P, C], U32, name="cw_deal", align_bytes=64)
@@ -98,40 +105,37 @@ def tile_picked_candundergspan_none_po_kernel(
         nc.vector.tensor_copy(cw_deal[:].rearrange("p (t m) -> p t m", t=PACK), xc_w[:].rearrange("p (m t) -> p t m", t=PACK))
         nc.vector.tensor_copy(cs_deal[:].rearrange("p (t m) -> p t m", t=PACK), xc_s[:].rearrange("p (m t) -> p t m", t=PACK))
 
-        last0, last_n = Z_CHUNKS[-1]
+        last0 = Z_CHUNKS[-1][0]
         neg_gs = keep.tile([P, 1], F32, name="neg_gs")
-        gy_last = keep.tile([P, last_n], F32, name="gy_last")
-        nc.vector.tensor_scalar(neg_gs[:], gs_sb[:, PACK - 1 : PACK], -1.0, None, ALU.mult)
-        nc.vector.tensor_scalar(gy_last[:], y_sb[PACK - 1][:, last0:], gs_sb[:, PACK - 1 : PACK], None, ALU.mult)
+        gy_last = keep.tile([P, S], F32, name="gy_last")
+        nc.vector.tensor_scalar(neg_gs[:], gs_sb[:, last_t:], -1.0, None, ALU.mult)
+        nc.vector.tensor_scalar(gy_last[:], y_sb[last_t][:], gs_sb[:, last_t:], None, ALU.mult)
         z_w = keep.tile([P, S], U32, name="z_w", align_bytes=64)
         z_s = keep.tile([P, S], U8, name="z_s", align_bytes=64)
         s_ps = [psum.tile([P, S], F32, name="s_ps%d" % t) for t in range(PACK)]
+        near = keep.tile([P, PACK, 2, S], F32, name="near")
+        low = keep.tile([P, PACK, S], F32, name="low")
+        z_all = keep.tile([P, S, PACK], BF16, name="z_all", align_bytes=64)
+        for t in range(last_t):
+            nc.scalar.activation(near[:, t, 0, :], y_sb[t][:].indirect(n1_sb[:]), COPY)
+            nc.scalar.activation(near[:, t, 1, :], y_sb[t][:].indirect(n2_sb[:]), COPY)
+            nc.vector.tensor_tensor(low[:, t, :], near[:, t, 0, :], near[:, t, 1, :], ALU.min)
+            nc.vector.tensor_tensor(low[:, t, :], y_sb[t][:, :S], low[:, t, :], ALU.subtract)
         for c0, n in Z_CHUNKS:
             cols = slice(c0, c0 + n)
             lists = slice(c0 // 16, (c0 + n) // 16)
-            near = keep.tile([P, PACK, 2, n], F32, name="near%d" % c0)
-            low = keep.tile([P, PACK, n], F32, name="low", tag="low")
-            z_bf = keep.tile([P, n, PACK], BF16, name="z_bf%d" % c0, align_bytes=64)
-            groups = ((0, 2), (2, 4)) if c0 + n < S else ((0, 2), (2, 3), (3, 4))
-            for t0, t1 in groups:
-                for t in range(t0, t1):
-                    nc.scalar.activation(near[:, t, 0, :], y_sb[t][:].indirect(n1_sb[:, lists]), COPY)
-                    nc.scalar.activation(near[:, t, 1, :], y_sb[t][:].indirect(n2_sb[:, lists]), COPY)
-                nc.vector.tensor_tensor(low[:, t0:t1, :], near[:, t0:t1, 0, :], near[:, t0:t1, 1, :], ALU.min)
-                if c0 == last0 and t1 == PACK:
-                    nc.vector.scalar_tensor_tensor(z_bf[:, :, t0], low[:, t0, :], neg_gs[:], gy_last[:], ALU.mult, ALU.add)
-                    continue
-                for t in range(t0, t1):
-                    nc.vector.tensor_tensor(low[:, t, :], y_sb[t][:, cols], low[:, t, :], ALU.subtract)
-                tn = PACK - 1 if c0 == last0 else PACK
-                if t1 == tn:
-                    nc.vector.tensor_tensor(
-                        z_bf[:, :, :tn],
-                        low[:, :tn].rearrange("p t j -> p j t"),
-                        gs_sb[:, :tn].unsqueeze(1).to_broadcast([P, n, tn]),
-                        ALU.mult,
-                    )
-            nc.vector.quantize_mx(out=z_w[:, cols].bitcast(FP8X4), scales=z_s[:, cols], in_=z_bf[:].rearrange("p j t -> p (j t)"))
+            z_bf = z_all[:, cols]
+            nc.vector.tensor_tensor(
+                z_bf[:, :, :last_t],
+                low[:, :last_t, cols].rearrange("p t j -> p j t"),
+                gs_sb[:, :last_t].unsqueeze(1).to_broadcast([P, n, last_t]),
+                ALU.mult,
+            )
+            nc.scalar.activation(near[:, last_t, 0, cols], y_sb[last_t][:].indirect(n1_sb[:, lists]), COPY)
+            nc.scalar.activation(near[:, last_t, 1, cols], y_sb[last_t][:].indirect(n2_sb[:, lists]), COPY)
+            nc.vector.tensor_tensor(low[:, last_t, cols], near[:, last_t, 0, cols], near[:, last_t, 1, cols], ALU.min)
+            nc.vector.scalar_tensor_tensor(z_bf[:, :, last_t], low[:, last_t, cols], neg_gs[:], gy_last[:, cols], ALU.mult, ALU.add)
+            nc.vector.quantize_mx(out=z_w[:, cols].bitcast(FP8X4), scales=z_s[:, cols], in_=z_bf.rearrange("p j t -> p (j t)"))
             for t in range(PACK):
                 nc.tensor.matmul_mx(
                     out=s_ps[t][:, cols],
@@ -162,8 +166,8 @@ def tile_picked_candundergspan_none_po_kernel(
             mn = keep.tile([P, PACK, n], F32, name="mn%d" % c0)
             res = keep.tile([P, PACK, n], F32, name="res%d" % c0)
             res_bf = keep.tile([P, n, PACK], BF16, name="res_bf%d" % c0, align_bytes=64)
-            pair_groups = ((0, 1), (1, 2), (2, 3), (3, 4)) if n == 128 else ((0, 2), (2, 4)) if c0 + n < S else ((0, 2), (2, 3), (3, 4))
-            end_groups = ((0, 2), (2, 4)) if n == 128 else ((0, 4),) if c0 + n < S else ((0, 3), (3, 4))
+            pair_groups = ((0, 1), (1, 2), (2, 3), (3, 4)) if c0 + n < S else ((0, 2), (2, 3), (3, 4))
+            end_groups = ((0, 2), (2, 4)) if c0 + n < S else ((0, 3), (3, 4))
             for e0, e1 in end_groups:
                 for t0, t1 in pair_groups:
                     if e0 <= t0 < e1:

@@ -20,8 +20,8 @@ P = 128
 PACK = 4
 MEMBERS = 4
 Z_CHUNKS = ((0, 128), (128, 128))
-OUT_CHUNKS = ((0, 64), (64, 128), (192, 64))
-S_WINDOW = 512 + 16
+OUT_CHUNKS = ((0, 64), (64, 64), (128, 64), (192, 64))
+S_WINDOW = 256 + 16
 
 
 def tile_picked_candundergspan_none_po_kernel(
@@ -43,9 +43,8 @@ def tile_picked_candundergspan_none_po_kernel(
         gs_sb = keep.tile([P, PACK], F32, name="gs_sb")
         ws_raw = keep.tile([P, H], U8, name="ws_raw", align_bytes=64)
 
-        nc.vector.memset(xs_tab[:, : T // 2].bitcast(I32), 0)
-        nc.gpsimd.memset(xs_tab[:, T // 2 :].bitcast(I32), 0)
         nc.gpsimd.memset(ws_raw[:].bitcast(I32), 0)
+        nc.vector.memset(xs_tab[:].bitcast(I32), 0)
         nc.sync.dma_start(offs_sb[:], offs)
         nc.sync.dma_start(w_raw[:].bitcast(I32), w1_words[0].bitcast(I32))
         nc.sync.dma_start(cand_sb[:], cand)
@@ -54,9 +53,9 @@ def tile_picked_candundergspan_none_po_kernel(
             nc.sync.dma_start(tile_sb[:], src)
         nc.sync.dma_start(gs_sb[:], gs.rearrange("(p t) o -> p (t o)", t=PACK))
         for q in range(4):
-            nc.scalar.dma_start(xs_tab[32 * q : 32 * q + 4, :].bitcast(I32), x_scales[0, 4 * q : 4 * q + 4, :].bitcast(I32))
-        for q in range(4):
             nc.scalar.dma_start(ws_raw[32 * q : 32 * q + 4, :].bitcast(I32), w1_scales[0, 4 * q : 4 * q + 4, :].bitcast(I32))
+        for q in range(4):
+            nc.scalar.dma_start(xs_tab[32 * q : 32 * q + 4, :].bitcast(I32), x_scales[0, 4 * q : 4 * q + 4, :].bitcast(I32))
 
         s_sb = [keep.tile([P, S_WINDOW], F32, name="s_sb%d" % t) for t in range(PACK)]
         for t in range(PACK):
@@ -72,12 +71,12 @@ def tile_picked_candundergspan_none_po_kernel(
         nc.vector.tensor_copy(w_first[:].rearrange("p (m b) -> p m b", b=2), w_cols[:, 0])
         nc.vector.tensor_copy(w_rest[:].rearrange("p t (m b) -> p t m b", b=2), w_cols[:, 1:])
         nc.vector.tensor_copy(ws_deal[:].rearrange("p (t m) -> p t m", t=PACK), ws_raw[:].rearrange("p (m t) -> p t m", t=PACK))
-        nc.vector.tensor_copy(xq_s[:], xs_tab[:].indirect(offs_sb[:]))
         nc.vector.tensor_copy(xq_w[:], x_tab[:].bitcast(U32).indirect(offs_sb[:]))
+        nc.vector.tensor_copy(xq_s[:], xs_tab[:].indirect(offs_sb[:]))
 
         last_t = PACK - 1
-        y_sb = [keep.tile([P, 2 * S if t < last_t else S], F32, name="y_sb%d" % t) for t in range(PACK)]
-        for t in range(last_t):
+        y_sb = [keep.tile([P, 2 * S if t < 2 else S], F32, name="y_sb%d" % t) for t in range(PACK)]
+        for t in range(2):
             nc.vector.memset(y_sb[t][:, S:], 0.0)
         y_ps = [psum.tile([P, S], F32, name="y_ps%d" % t) for t in range(PACK)]
         for t in range(PACK):
@@ -100,41 +99,47 @@ def tile_picked_candundergspan_none_po_kernel(
         xc_w = keep.tile([P, C], U32, name="xc_w", tag="scales_then_words", align_bytes=64)
         cs_deal = keep.tile([P, C], U8, name="cs_deal", align_bytes=64)
         cw_deal = keep.tile([P, C], U32, name="cw_deal", align_bytes=64)
-        nc.vector.tensor_copy(xc_w[:], x_tab[:].bitcast(U32).indirect(cand_sb[:]))
         nc.vector.tensor_copy(xc_s[:], xs_tab[:].indirect(cand_sb[:]))
+        nc.vector.tensor_copy(xc_w[:], x_tab[:].bitcast(U32).indirect(cand_sb[:]))
         nc.vector.tensor_copy(cw_deal[:].rearrange("p (t m) -> p t m", t=PACK), xc_w[:].rearrange("p (m t) -> p t m", t=PACK))
         nc.vector.tensor_copy(cs_deal[:].rearrange("p (t m) -> p t m", t=PACK), xc_s[:].rearrange("p (m t) -> p t m", t=PACK))
 
         last0 = Z_CHUNKS[-1][0]
-        neg_gs = keep.tile([P, 1], F32, name="neg_gs")
-        gy_last = keep.tile([P, S], F32, name="gy_last")
-        nc.vector.tensor_scalar(neg_gs[:], gs_sb[:, last_t:], -1.0, None, ALU.mult)
-        nc.vector.tensor_scalar(gy_last[:], y_sb[last_t][:], gs_sb[:, last_t:], None, ALU.mult)
         z_w = keep.tile([P, S], U32, name="z_w", align_bytes=64)
         z_s = keep.tile([P, S], U8, name="z_s", align_bytes=64)
         s_ps = [psum.tile([P, S], F32, name="s_ps%d" % t) for t in range(PACK)]
         near = keep.tile([P, PACK, 2, S], F32, name="near")
         low = keep.tile([P, PACK, S], F32, name="low")
         z_all = keep.tile([P, S, PACK], BF16, name="z_all", align_bytes=64)
-        for t in range(last_t):
-            nc.scalar.activation(near[:, t, 0, :], y_sb[t][:].indirect(n1_sb[:]), COPY)
-            nc.scalar.activation(near[:, t, 1, :], y_sb[t][:].indirect(n2_sb[:]), COPY)
-            nc.vector.tensor_tensor(low[:, t, :], near[:, t, 0, :], near[:, t, 1, :], ALU.min)
-            nc.vector.tensor_tensor(low[:, t, :], y_sb[t][:, :S], low[:, t, :], ALU.subtract)
-        for c0, n in Z_CHUNKS:
+
+        def make_diff(ts, c0, n):
             cols = slice(c0, c0 + n)
             lists = slice(c0 // 16, (c0 + n) // 16)
-            z_bf = z_all[:, cols]
+            for t in range(ts.start, ts.stop):
+                nc.scalar.activation(near[:, t, 0, cols], y_sb[t][:].indirect(n1_sb[:, lists]), COPY)
+                nc.scalar.activation(near[:, t, 1, cols], y_sb[t][:].indirect(n2_sb[:, lists]), COPY)
+                nc.vector.tensor_tensor(low[:, t, cols], near[:, t, 0, cols], near[:, t, 1, cols], ALU.min)
+                nc.vector.tensor_tensor(low[:, t, cols], y_sb[t][:, cols], low[:, t, cols], ALU.subtract)
+
+        def apply_gain(ts, c0, n):
+            cols = slice(c0, c0 + n)
             nc.vector.tensor_tensor(
-                z_bf[:, :, :last_t],
-                low[:, :last_t, cols].rearrange("p t j -> p j t"),
-                gs_sb[:, :last_t].unsqueeze(1).to_broadcast([P, n, last_t]),
+                z_all[:, cols, ts],
+                low[:, ts, cols].rearrange("p t j -> p j t"),
+                gs_sb[:, ts].unsqueeze(1).to_broadcast([P, n, 2]),
                 ALU.mult,
             )
-            nc.scalar.activation(near[:, last_t, 0, cols], y_sb[last_t][:].indirect(n1_sb[:, lists]), COPY)
-            nc.scalar.activation(near[:, last_t, 1, cols], y_sb[last_t][:].indirect(n2_sb[:, lists]), COPY)
-            nc.vector.tensor_tensor(low[:, last_t, cols], near[:, last_t, 0, cols], near[:, last_t, 1, cols], ALU.min)
-            nc.vector.scalar_tensor_tensor(z_bf[:, :, last_t], low[:, last_t, cols], neg_gs[:], gy_last[:, cols], ALU.mult, ALU.add)
+
+        make_diff(slice(0, 2), 0, S)
+        apply_gain(slice(0, 2), 0, last0)
+        for c0, n in Z_CHUNKS:
+            cols = slice(c0, c0 + n)
+            z_bf = z_all[:, cols]
+            make_diff(slice(2, 4), c0, n)
+            apply_gain(slice(2, 4), c0, n)
+            if c0 == last0:
+                for t in range(2):
+                    nc.scalar.activation(z_all[:, cols, t], low[:, t, cols], COPY, scale=gs_sb[:, t : t + 1])
             nc.vector.quantize_mx(out=z_w[:, cols].bitcast(FP8X4), scales=z_s[:, cols], in_=z_bf.rearrange("p j t -> p (j t)"))
             for t in range(PACK):
                 nc.tensor.matmul_mx(
@@ -166,7 +171,7 @@ def tile_picked_candundergspan_none_po_kernel(
             mn = keep.tile([P, PACK, n], F32, name="mn%d" % c0)
             res = keep.tile([P, PACK, n], F32, name="res%d" % c0)
             res_bf = keep.tile([P, n, PACK], BF16, name="res_bf%d" % c0, align_bytes=64)
-            pair_groups = ((0, 1), (1, 2), (2, 3), (3, 4)) if c0 + n < S else ((0, 2), (2, 3), (3, 4))
+            pair_groups = ((0, 1), (1, 2), (2, 3), (3, 4)) if c0 == 0 else ((0, 2), (2, 4)) if c0 + n < S else ((0, 2), (2, 3), (3, 4))
             end_groups = ((0, 2), (2, 4)) if c0 + n < S else ((0, 3), (3, 4))
             for e0, e1 in end_groups:
                 for t0, t1 in pair_groups:

@@ -130,14 +130,26 @@ def tile_picked_candundergspan_none_po_kernel(
                 ALU.mult,
             )
 
+        neg_gain = keep.tile([P, 1], F32, name="neg_gain")
+        gained_y = keep.tile([P, S - last0], F32, name="gained_y")
+        nc.vector.tensor_scalar(neg_gain[:], gs_sb[:, last_t:], -1.0, None, ALU.mult)
+        nc.vector.tensor_scalar(gained_y[:], y_sb[last_t][:, last0:], gs_sb[:, last_t:], None, ALU.mult)
         make_diff(slice(0, 2), 0, S)
         apply_gain(slice(0, 2), 0, last0)
         for c0, n in Z_CHUNKS:
             cols = slice(c0, c0 + n)
             z_bf = z_all[:, cols]
-            make_diff(slice(2, 4), c0, n)
-            apply_gain(slice(2, 4), c0, n)
-            if c0 == last0:
+            if c0 < last0:
+                make_diff(slice(2, 4), c0, n)
+                apply_gain(slice(2, 4), c0, n)
+            else:
+                lists = slice(c0 // 16, (c0 + n) // 16)
+                make_diff(slice(2, 3), c0, n)
+                nc.vector.tensor_scalar(z_all[:, cols, 2], low[:, 2, cols], gs_sb[:, 2:3], None, ALU.mult)
+                nc.scalar.activation(near[:, 3, 0, cols], y_sb[3][:].indirect(n1_sb[:, lists]), COPY)
+                nc.scalar.activation(near[:, 3, 1, cols], y_sb[3][:].indirect(n2_sb[:, lists]), COPY)
+                nc.vector.tensor_tensor(low[:, 3, cols], near[:, 3, 0, cols], near[:, 3, 1, cols], ALU.min)
+                nc.vector.scalar_tensor_tensor(z_all[:, cols, 3], low[:, 3, cols], neg_gain[:], gained_y[:], ALU.mult, ALU.add)
                 for t in range(2):
                     nc.scalar.activation(z_all[:, cols, t], low[:, t, cols], COPY, scale=gs_sb[:, t : t + 1])
             nc.vector.quantize_mx(out=z_w[:, cols].bitcast(FP8X4), scales=z_s[:, cols], in_=z_bf.rearrange("p j t -> p (j t)"))

from contextlib import ExitStack

import concourse.mybir as mybir

K, T, S, H, C, W = 512, 2048, 256, 512, 512, 1024
FLOPS = 2 * K * H * S + 2 * K * C * S

F32 = mybir.dt.float32
BF16 = mybir.dt.bfloat16
I32 = mybir.dt.int32
U32 = mybir.dt.uint32
U16 = mybir.dt.uint16
U8 = mybir.dt.uint8
FP8X4 = mybir.dt.float8_e4m3fn_x4
FP4X4 = mybir.dt.float4_e2m1fn_x4
ALU = mybir.AluOpType
COPY = mybir.ActivationFunctionType.Copy

P = 128
PACK = 4
MEMBERS = 4
Z_CHUNKS = ((0, 128), (128, 128))
OUT_CHUNKS = ((0, 64), (64, 64), (128, 64), (192, 64))
S_WINDOW = 256 + 16


def tile_picked_candundergspan_none_po_kernel(
    tc, x_words, x_scales, w1_words, w1_scales, gs, offs, n1, n2, cand, n3, out_0, out_1, out_2
):
    nc = tc.nc
    with ExitStack() as ctx:
        keep = ctx.enter_context(tc.tile_pool(name="keep", bufs=1))
        psum = ctx.enter_context(tc.psum_pool(name="psum", bufs=1))

        offs_sb = keep.tile([P, S // 16], U16, name="offs_sb")
        cand_sb = keep.tile([P, C // 16], U16, name="cand_sb")
        n1_sb = keep.tile([P, S // 16], U16, name="n1_sb")
        n2_sb = keep.tile([P, S // 16], U16, name="n2_sb")
        n3_sb = keep.tile([P, W // 16], U16, name="n3_sb")
        x_tab = keep.tile([P, T], I32, name="x_tab", align_bytes=64)
        xs_tab = keep.tile([P, T], U8, name="xs_tab", align_bytes=64)
        w_raw = keep.tile([P, 2 * H], U8, name="w_raw", align_bytes=64)
        gs_sb = keep.tile([P, PACK], F32, name="gs_sb")
        ws_raw = keep.tile([P, H], U8, name="ws_raw", align_bytes=64)

        nc.gpsimd.memset(ws_raw[:].bitcast(I32), 0)
        nc.vector.memset(xs_tab[:].bitcast(I32), 0)
        nc.sync.dma_start(offs_sb[:], offs)
        nc.sync.dma_start(w_raw[:].bitcast(I32), w1_words[0].bitcast(I32))
        nc.sync.dma_start(cand_sb[:], cand)
        nc.sync.dma_start(x_tab[:], x_words[0].rearrange("p n t -> p (n t)").bitcast(I32))
        for tile_sb, src in ((n1_sb, n1), (n2_sb, n2), (n3_sb, n3)):
            nc.sync.dma_start(tile_sb[:], src)
        nc.sync.dma_start(gs_sb[:], gs.rearrange("(p t) o -> p (t o)", t=PACK))
        for q in range(4):
            nc.scalar.dma_start(ws_raw[32 * q : 32 * q + 4, :].bitcast(I32), w1_scales[0, 4 * q : 4 * q + 4, :].bitcast(I32))
        for q in range(4):
            nc.scalar.dma_start(xs_tab[32 * q : 32 * q + 4, :].bitcast(I32), x_scales[0, 4 * q : 4 * q + 4, :].bitcast(I32))

        s_sb = [keep.tile([P, S_WINDOW], F32, name="s_sb%d" % t) for t in range(PACK)]
        for t in range(PACK):
            nc.gpsimd.memset(s_sb[t][:, S:], 0.0)

        xq_s = keep.tile([P, S], U8, name="xq_s", align_bytes=64)
        xq_w = keep.tile([P, S], U32, name="xq_w", align_bytes=64)
        w_first = keep.tile([P, 2 * P], U8, name="w_first", tag="scales_then_words", align_bytes=64)
        w_rest = keep.tile([P, PACK - 1, 2 * P], U8, name="w_rest", align_bytes=64)
        w_deal = [w_first[:]] + [w_rest[:, t] for t in range(PACK - 1)]
        ws_deal = keep.tile([P, H], U8, name="ws_deal", align_bytes=64)
        w_cols = w_raw[:].rearrange("p (m t b) -> p t m b", t=PACK, b=2)
        nc.vector.tensor_copy(w_first[:].rearrange("p (m b) -> p m b", b=2), w_cols[:, 0])
        nc.vector.tensor_copy(w_rest[:].rearrange("p t (m b) -> p t m b", b=2), w_cols[:, 1:])
        nc.vector.tensor_copy(ws_deal[:].rearrange("p (t m) -> p t m", t=PACK), ws_raw[:].rearrange("p (m t) -> p t m", t=PACK))
        nc.vector.tensor_copy(xq_w[:], x_tab[:].bitcast(U32).indirect(offs_sb[:]))
        nc.vector.tensor_copy(xq_s[:], xs_tab[:].indirect(offs_sb[:]))

        last_t = PACK - 1
        y_sb = [keep.tile([P, 2 * S if t < 2 else S], F32, name="y_sb%d" % t) for t in range(PACK)]
        for t in range(2):
            nc.vector.memset(y_sb[t][:, S:], 0.0)
        y_ps = [psum.tile([P, S], F32, name="y_ps%d" % t) for t in range(PACK)]
        for t in range(PACK):
            nc.tensor.matmul_mx(
                out=y_ps[t][:],
                lhsT=w_deal[t].bitcast(FP4X4),
                lhsT_scale=ws_deal[:, P * t : P * (t + 1)],
                rhs=xq_w[:].bitcast(FP8X4),
                rhs_scale=xq_s[:],
                start=True,
                stop=True,
            )
        for t in range(PACK):
            if t < 2:
                nc.scalar.copy(y_sb[t][:, :S], y_ps[t][:])
            else:
                nc.vector.tensor_copy(y_sb[t][:, :S], y_ps[t][:])

        xc_s = keep.tile([P, C], U8, name="xc_s", align_bytes=64)
        xc_w = keep.tile([P, C], U32, name="xc_w", tag="scales_then_words", align_bytes=64)
        cs_deal = keep.tile([P, C], U8, name="cs_deal", align_bytes=64)
        cw_deal = keep.tile([P, C], U32, name="cw_deal", align_bytes=64)
        nc.vector.tensor_copy(xc_s[:], xs_tab[:].indirect(cand_sb[:]))
        nc.vector.tensor_copy(xc_w[:], x_tab[:].bitcast(U32).indirect(cand_sb[:]))
        nc.vector.tensor_copy(cw_deal[:].rearrange("p (t m) -> p t m", t=PACK), xc_w[:].rearrange("p (m t) -> p t m", t=PACK))
        nc.vector.tensor_copy(cs_deal[:].rearrange("p (t m) -> p t m", t=PACK), xc_s[:].rearrange("p (m t) -> p t m", t=PACK))

        last0 = Z_CHUNKS[-1][0]
        z_w = keep.tile([P, S], U32, name="z_w", align_bytes=64)
        z_s = keep.tile([P, S], U8, name="z_s", align_bytes=64)
        s_ps = [psum.tile([P, S], F32, name="s_ps%d" % t) for t in range(PACK)]
        near = keep.tile([P, PACK, 2, S], F32, name="near")
        low = keep.tile([P, PACK, S], F32, name="low")
        z_all = keep.tile([P, S, PACK], BF16, name="z_all", align_bytes=64)

        def make_diff(ts, c0, n):
            cols = slice(c0, c0 + n)
            lists = slice(c0 // 16, (c0 + n) // 16)
            for t in range(ts.start, ts.stop):
                nc.scalar.activation(near[:, t, 0, cols], y_sb[t][:].indirect(n1_sb[:, lists]), COPY)
                nc.scalar.activation(near[:, t, 1, cols], y_sb[t][:].indirect(n2_sb[:, lists]), COPY)
                nc.vector.tensor_tensor(low[:, t, cols], near[:, t, 0, cols], near[:, t, 1, cols], ALU.min)
                nc.vector.tensor_tensor(low[:, t, cols], y_sb[t][:, cols], low[:, t, cols], ALU.subtract)

        def apply_gain(ts, c0, n):
            cols = slice(c0, c0 + n)
            nc.vector.tensor_tensor(
                z_all[:, cols, ts],
                low[:, ts, cols].rearrange("p t j -> p j t"),
                gs_sb[:, ts].unsqueeze(1).to_broadcast([P, n, 2]),
                ALU.mult,
            )

        neg_gain = keep.tile([P, 1], F32, name="neg_gain")
        gained_y = keep.tile([P, S - last0], F32, name="gained_y")
        nc.vector.tensor_scalar(neg_gain[:], gs_sb[:, last_t:], -1.0, None, ALU.mult)
        nc.vector.tensor_scalar(gained_y[:], y_sb[last_t][:, last0:], gs_sb[:, last_t:], None, ALU.mult)
        make_diff(slice(0, 2), 0, S)
        apply_gain(slice(0, 2), 0, last0)
        for c0, n in Z_CHUNKS:
            cols = slice(c0, c0 + n)
            z_bf = z_all[:, cols]
            if c0 < last0:
                make_diff(slice(2, 4), c0, n)
                apply_gain(slice(2, 4), c0, n)
            else:
                lists = slice(c0 // 16, (c0 + n) // 16)
                make_diff(slice(2, 3), c0, n)
                nc.vector.tensor_scalar(z_all[:, cols, 2], low[:, 2, cols], gs_sb[:, 2:3], None, ALU.mult)
                nc.scalar.activation(near[:, 3, 0, cols], y_sb[3][:].indirect(n1_sb[:, lists]), COPY)
                nc.scalar.activation(near[:, 3, 1, cols], y_sb[3][:].indirect(n2_sb[:, lists]), COPY)
                nc.vector.tensor_tensor(low[:, 3, cols], near[:, 3, 0, cols], near[:, 3, 1, cols], ALU.min)
                nc.vector.scalar_tensor_tensor(z_all[:, cols, 3], low[:, 3, cols], neg_gain[:], gained_y[:], ALU.mult, ALU.add)
                for t in range(2):
                    nc.scalar.activation(z_all[:, cols, t], low[:, t, cols], COPY, scale=gs_sb[:, t : t + 1])
            nc.vector.quantize_mx(out=z_w[:, cols].bitcast(FP8X4), scales=z_s[:, cols], in_=z_bf.rearrange("p j t -> p (j t)"))
            for t in range(PACK):
                nc.tensor.matmul_mx(
                    out=s_ps[t][:, cols],
                    lhsT=cw_deal[:, P * t : P * (t + 1)].bitcast(FP8X4),
                    lhsT_scale=cs_deal[:, P * t : P * (t + 1)],
                    rhs=z_w[:, cols].bitcast(FP8X4),
                    rhs_scale=z_s[:, cols],
                    start=True,
                    stop=True,
                )
        for c0, n in Z_CHUNKS[:-1]:
            for t in range(PACK):
                nc.scalar.activation(s_sb[t][:, c0 : c0 + n], s_ps[t][:, c0 : c0 + n], COPY, scale=0.0625)
        for t in range(PACK):
            nc.vector.tensor_scalar(s_sb[t][:, last0:S], s_ps[t][:, last0:S], 0.0625, None, ALU.mult)

        o_w = keep.tile([P, S], U32, name="o_w", align_bytes=64)
        o_s = keep.tile([P, S], U8, name="o_s", align_bytes=64)
        out_rows = out_0.rearrange("(p t) j -> p t j", t=PACK)
        out_words = out_1[0].rearrange("p n t -> p (n t)").bitcast(I32)
        for c0, n in OUT_CHUNKS:
            cols = slice(c0, c0 + n)
            lists = slice(c0 * MEMBERS // 16, (c0 + n) * MEMBERS // 16)
            mb = keep.tile([P, PACK, n, MEMBERS], F32, name="mb%d" % c0)
            hi = keep.tile([P, PACK, n, 2], F32, name="hi%d" % c0)
            lo = keep.tile([P, PACK, n, 2], F32, name="lo%d" % c0)
            mx = keep.tile([P, PACK, n], F32, name="mx%d" % c0)
            mn = keep.tile([P, PACK, n], F32, name="mn%d" % c0)
            res = keep.tile([P, PACK, n], F32, name="res%d" % c0)
            res_bf = keep.tile([P, n, PACK], BF16, name="res_bf%d" % c0, align_bytes=64)
            pair_groups = ((0, 1), (1, 2), (2, 3), (3, 4)) if c0 == 0 else ((0, 2), (2, 4)) if c0 + n < S else ((0, 2), (2, 3), (3, 4))
            end_groups = ((0, 2), (2, 4)) if c0 + n < S else ((0, 3), (3, 4))
            for e0, e1 in end_groups:
                for t0, t1 in pair_groups:
                    if e0 <= t0 < e1:
                        for t in range(t0, t1):
                            nc.scalar.activation(mb[:, t].rearrange("p j m -> p (j m)"), s_sb[t][:].indirect(n3_sb[:, lists]), COPY)
                        ts = slice(t0, t1)
                        nc.vector.tensor_tensor(hi[:, ts], mb[:, ts, :, 0:2], mb[:, ts, :, 2:4], ALU.max)
                        nc.vector.tensor_tensor(lo[:, ts], mb[:, ts, :, 0:2], mb[:, ts, :, 2:4], ALU.min)
                ts = slice(e0, e1)
                nc.vector.tensor_tensor(mx[:, ts], hi[:, ts, :, 0], hi[:, ts, :, 1], ALU.max)
                nc.vector.tensor_tensor(mn[:, ts], lo[:, ts, :, 0], lo[:, ts, :, 1], ALU.min)
                if c0 + n == S and e1 == PACK:
                    nc.vector.scalar_tensor_tensor(res_bf[:, :, e0], mn[:, e0], -0.5, mx[:, e0], ALU.mult, ALU.add)
                nc.vector.scalar_tensor_tensor(res[:, ts], mn[:, ts], -0.5, mx[:, ts], ALU.mult, ALU.add)
                tn = PACK - 1 if c0 + n == S else PACK
                if e1 == tn:
                    nc.vector.tensor_copy(res_bf[:, :, :tn], res[:, :tn].rearrange("p t j -> p j t"))
            nc.sync.dma_start(out_rows[:, :, cols], res[:])
            nc.vector.quantize_mx(out=o_w[:, cols].bitcast(FP8X4), scales=o_s[:, cols], in_=res_bf[:].rearrange("p j t -> p (j t)"))
            nc.sync.dma_start(out_words[:, cols], o_w[:, cols].bitcast(I32))
        for q in range(4):
            eng = nc.sync if q % 2 else nc.scalar
            eng.dma_start(out_2[0, 4 * q : 4 * q + 4, :].bitcast(I32), o_s[32 * q : 32 * q + 4, :].bitcast(I32))
